import numpy as np
import ml_dtypes


def mxq(x, axis, fmt="e4m3"):
    dtype, down = {"e4m3": (ml_dtypes.float8_e4m3fn, 7), "e5m2": (ml_dtypes.float8_e5m2, 14)}[fmt]
    v = np.moveaxis(np.asarray(x, np.float32).astype(ml_dtypes.bfloat16).astype(np.float64), axis, -1)
    blocks = v.reshape(v.shape[:-1] + (-1, 32))
    amax = np.abs(blocks).max(-1, keepdims=True)
    byte = np.maximum(np.where(amax > 0, np.frexp(amax)[1] - 1 + 127, 0) - down, 1)
    scale = np.exp2(byte - 127.0)
    codes = (blocks / scale).astype(np.float32).astype(dtype).astype(np.float64)
    return np.moveaxis((codes * scale).reshape(v.shape), -1, axis)


WIDE = False


def mx_kscale(k):
    if not WIDE:
        return np.ones(k)
    levels = np.array([10, -10, 5, -5, 0])
    if k % 512:
        return np.exp2(np.random.permutation(np.resize(levels, k // 32))).repeat(32)
    a = np.empty((k // 512, 16))
    for p in range(k // 512):
        a[p, :8] = np.random.permutation(np.resize(levels, 8))
        for g in range(8):
            far = levels[np.abs(levels - a[p, g]) >= 10]
            a[p, g + 8] = far[np.random.randint(len(far))]
    return np.exp2(a.ravel()).repeat(32)


def f64(x):
    return np.asarray(x).astype(np.float64)


def striped(idx):
    return np.tile(idx.reshape(-1, 16).T, (8, 1)).astype(np.uint16)


def unstriped(offs):
    return offs[:16].T.reshape(-1).astype(np.int64)


E2M1 = np.array([0.0, 0.5, 1.0, 1.5, 2.0, 3.0, 4.0, 6.0, -0.0, -0.5, -1.0, -1.5, -2.0, -3.0, -4.0, -6.0])


def pack_weight(w, fmt):
    k, n = w.shape
    w = f64(np.asarray(w, np.float32).astype(ml_dtypes.bfloat16)).reshape(k // 32, 32, n)
    amax = np.abs(w).max(1)
    if fmt == "e4m3":
        byte = np.frexp(amax)[1] - 1 + 127 - 7
    else:
        mant, ex = np.frexp(amax / 6.0)
        byte = np.where(mant > 0.5, ex, ex - 1) + 127
    byte = np.clip(np.where(amax > 0, byte, 1), 1, 254)
    scaled = (w * np.exp2(127.0 - byte)[:, None, :]).reshape(k, n).astype(np.float32)
    by_word = np.ascontiguousarray(scaled.reshape(k // 512, 128, 4, n).transpose(0, 1, 3, 2))
    if fmt == "e4m3":
        words = by_word.astype(ml_dtypes.float8_e4m3fn).view(np.uint8)
    else:
        c = by_word.astype(ml_dtypes.float4_e2m1fn).view(np.uint8) & 0xF
        words = (c[..., 0::2] | (c[..., 1::2] << 4)).reshape(k // 512, 128, 2 * n)
    return np.ascontiguousarray(words), np.ascontiguousarray(byte.astype(np.uint8).reshape(k // 512, 16, n))


def unpack_weight(words, scales, fmt):
    g, _, n = scales.shape
    words = np.ascontiguousarray(words).reshape(g, 128, n, -1)
    if fmt == "e4m3":
        vals = words.view(ml_dtypes.float8_e4m3fn).astype(np.float64)
    else:
        nib = np.empty((g, 128, n, 4), np.uint8)
        nib[..., 0::2] = words & 0xF
        nib[..., 1::2] = words >> 4
        vals = E2M1[nib]
    vals = vals * np.repeat(np.exp2(scales.astype(np.float64) - 127.0), 8, axis=1)[..., None]
    return vals.transpose(0, 1, 3, 2).reshape(g * 512, n)


def gelu(v):
    return 0.5 * v * (1.0 + np.tanh(np.sqrt(2.0 / np.pi) * (v + 0.044715 * v**3)))


K, H, T, S, P = 1536, 1024, 4096, 1024, 512

def setup_inputs():
    n = np.random.standard_normal
    s = mx_kscale(K)[:, None]
    u = mx_kscale(H)[:, None]
    tab_words, tab_scales = pack_weight(n((K, T)) * s, "e4m3")
    w4_words, w4_scales = pack_weight(1.4 * n((K, H)) / np.sqrt(K) / s, "e2m1")
    return {
        "tab_words": tab_words,
        "tab_scales": tab_scales,
        "offs": striped(np.random.permutation(T)[:S]),
        "pos1": striped(np.random.permutation(S)[:P]),
        "pos2": striped(np.random.permutation(S)[:P]),
        "w4_words": w4_words,
        "w4_scales": w4_scales,
        "gain": (np.exp(0.3 * n(H)) * u[:, 0]).astype(np.float32),
        "dep": (0.7 * n((H, P)) * u).astype(np.float32),
        "disc": (1.6 * n(H) / np.sqrt(H) / u[:, 0] ** 2).astype(np.float32),
        "col": np.exp(0.3 * n(P)).astype(np.float32),
        "row": (0.5 * n(P)).astype(np.float32),
    }

def reference(tab_words, tab_scales, offs, pos1, pos2, w4_words, w4_scales, gain, dep, disc, col, row):
    v = unpack_weight(tab_words, tab_scales, "e4m3")[:, unstriped(offs)]
    w4 = unpack_weight(w4_words, w4_scales, "e2m1")
    h = np.tanh(w4.T @ v) * f64(gain)[:, None]
    x1 = mxq(h[:, unstriped(pos1)], 0, "e4m3")
    d = mxq(f64(dep), 0, "e4m3")
    x2 = mxq(np.abs(h[:, unstriped(pos2)]) * f64(disc)[:, None], 0, "e4m3")
    e = x1.T @ x2 + d.T @ x2
    return np.tanh(e) * f64(col)[:, None] + f64(row)[None, :]

@@ -1,0 +1,293 @@
+from contextlib import ExitStack
+
+import concourse.mybir as mybir
+
+K, H, T, S, NP = 1536, 1024, 4096, 1024, 512
+FLOPS = 2 * K * H * S + 2 * 2 * H * NP * NP
+
+F32 = mybir.dt.float32
+BF16 = mybir.dt.bfloat16
+I32 = mybir.dt.int32
+U32 = mybir.dt.uint32
+U16 = mybir.dt.uint16
+U8 = mybir.dt.uint8
+FP8X4 = mybir.dt.float8_e4m3fn_x4
+FP4X4 = mybir.dt.float4_e2m1fn_x4
+ACT = mybir.ActivationFunctionType
+ALU = mybir.AluOpType
+
+P = 128
+PACK = 4
+PASSES1 = K // (P * PACK)
+PASSES2 = H // (P * PACK)
+BANK = 512
+SCALE_ROWS = 16
+ROW0 = 40
+RUN = 4
+
+
+def tile_list_claim_chart_scores_kernel(
+    tc, tab_words, tab_scales, offs, pos1, pos2, w4_words, w4_scales, gain, dep, disc, col, row, out
+):
+    nc = tc.nc
+    with ExitStack() as ctx:
+        lists = ctx.enter_context(tc.tile_pool(name="lists", bufs=1))
+        keep = ctx.enter_context(tc.tile_pool(name="keep", bufs=1))
+        psum = ctx.enter_context(tc.psum_pool(name="psum", bufs=1))
+
+        def sb(shape, dtype, name, tag=None):
+            return keep.tile(shape, dtype, name=name, tag=tag or name, align_bytes=64)
+
+        def bank(i, name):
+            return psum.tile([P, BANK], F32, name=name, tag="bank%d" % i)
+
+        offs_sb = lists.tile([P, S // 16], U16, name="offs_sb")
+        pos1_sb = lists.tile([P, NP // 16], U16, name="pos1_sb")
+        pos2_sb = lists.tile([P, NP // 16], U16, name="pos2_sb")
+        nc.sync.dma_start(offs_sb[:], offs)
+        nc.sync.dma_start(pos1_sb[:], pos1)
+        nc.sync.dma_start(pos2_sb[:], pos2)
+
+        n_rows = SCALE_ROWS * PASSES1
+        tab_sc = sb([P, T], U8, "tab_sc")
+        nc.vector.memset(tab_sc[:].bitcast(I32), 0)
+        nc.scalar.dma_start(
+            tab_sc[ROW0 : ROW0 + n_rows, :].bitcast(I32), tab_scales.rearrange("a q t -> q a t").bitcast(I32)
+        )
+        w_sc = sb([P, H], U8, "w_sc", tag="shareD")
+        nc.vector.memset(w_sc[:].bitcast(I32), 0)
+        nc.scalar.dma_start(
+            w_sc[ROW0 : ROW0 + n_rows, :].bitcast(I32), w4_scales.rearrange("a q c -> q a c").bitcast(I32)
+        )
+        planes = sb([P, PASSES1 * (S + H)], U8, "planes")
+        nc.vector.memset(planes[:].bitcast(I32), 0)
+
+        half = 2 * P * PACK
+
+        def load_w(b, tag):
+            raw = sb([P, PASSES1, half], U8, "w_raw%d" % b, tag=tag)
+            nc.sync.dma_start(
+                raw[:].bitcast(I32),
+                w4_words.rearrange("a p c -> p a c")[:, :, b * half : (b + 1) * half].bitcast(I32),
+            )
+            return raw
+
+        def deal_w(b, raw):
+            dealt = sb([P, PASSES1, half], U8, "w_dealt%d" % b)
+            for a in range(PASSES1):
+                nc.vector.tensor_copy(
+                    dealt[:, a, :].bitcast(U16).rearrange("p (t q) -> p t q", t=PACK),
+                    raw[:, a, :].bitcast(U16).rearrange("p (q t) -> p t q", t=PACK),
+                )
+            return dealt
+
+        def load_tab(a, tag):
+            words = sb([P, T], I32, "tab%d" % a, tag=tag)
+            nc.sync.dma_start(words[:], tab_words[a].rearrange("p t i -> p (t i)").bitcast(I32))
+            return words
+
+        w_raw0 = load_w(0, "shareB")
+        tabs = [load_tab(0, "tab0")]
+
+        gain_sb = sb([P, PASSES2, PACK], F32, "gain_sb")
+        disc_sb = sb([P, PASSES2, PACK], F32, "disc_sb")
+        col_sb = sb([P, NP // P], F32, "col_sb")
+        nc.gpsimd.dma_start(gain_sb[:], gain.rearrange("(b p t) -> p b t", p=P, t=PACK))
+        nc.gpsimd.dma_start(disc_sb[:], disc.rearrange("(b p t) -> p b t", p=P, t=PACK))
+        with nc.allow_non_contiguous_dma(reason="one value of col to a partition"):
+            nc.gpsimd.dma_start(col_sb[:], col.rearrange("(i p) -> p i", p=P))
+
+        w_dealt = [deal_w(0, w_raw0)]
+        tabs.append(load_tab(1, "shareB"))
+
+        picked_sc = sb([P, S], U8, "picked_sc")
+        nc.vector.tensor_copy(picked_sc[:], tab_sc[:].indirect(offs_sb[:]))
+        stage = sb([P, S + H], U8, "stage", tag="shareC")
+        nc.vector.tensor_copy(stage[:, :S].bitcast(I32), picked_sc[:].bitcast(I32))
+        nc.vector.tensor_copy(
+            stage[:, S:].rearrange("p (b t q) -> p b t q", b=PASSES2, t=PACK),
+            w_sc[:].rearrange("p (b q t) -> p b t q", b=PASSES2, t=PACK),
+        )
+        for quad in range(4):
+            src0 = ROW0 + 4 * PASSES1 * quad
+            nc.sync.dma_start(
+                planes[32 * quad : 32 * quad + 4, :].bitcast(I32).rearrange("r (a n) -> r a n", a=PASSES1),
+                stage[src0 : src0 + 4 * PASSES1, :].bitcast(I32),
+            )
+        tabs.append(load_tab(2, "shareD"))
+        w_raw1 = load_w(1, "shareC")
+
+        mag = sb([P, PASSES2 * PACK], F32, "mag")
+        gain_flat = gain_sb[:].rearrange("p b t -> p (b t)")
+        twice = sb([P, PASSES2 * PACK], F32, "twice")
+        nc.gpsimd.tensor_scalar(twice[:], gain_flat, 0.0, 2.0, ALU.max, ALU.mult)
+        nc.gpsimd.tensor_tensor(mag[:], twice[:], gain_flat, ALU.subtract)
+        weight2 = sb([P, PASSES2, PACK], F32, "weight2")
+        nc.gpsimd.tensor_tensor(
+            weight2[:].rearrange("p b t -> p (b t)"), mag[:], disc_sb[:].rearrange("p b t -> p (b t)"), ALU.mult
+        )
+
+        picked = {}
+        for a in range(PASSES1):
+            window = tabs[a][:].bitcast(U32)
+            if a < PASSES1 - 1:
+                g = sb([P, S], U32, "picked%d" % a)
+                nc.vector.tensor_copy(g[:], window.indirect(offs_sb[:]))
+                for c in range(2):
+                    picked[a, c] = g[:, c * BANK : (c + 1) * BANK]
+            else:
+                for c in range(2):
+                    g = sb([P, BANK], U32, "picked%d_%d" % (a, c))
+                    nc.vector.tensor_copy(g[:], window.indirect(offs_sb[:, c * 32 : (c + 1) * 32]))
+                    picked[a, c] = g[:]
+
+        dep_raw = []
+        for b, tag in enumerate(("shareB", "shareD")):
+            raw = sb([P, PACK, NP], F32, "dep_raw%d" % b, tag=tag)
+            nc.sync.dma_start(raw[:], dep[b * P * PACK : (b + 1) * P * PACK, :].rearrange("(p t) m -> p t m", t=PACK))
+            dep_raw.append(raw)
+
+        def mm1(acc, b, t, a, c):
+            base = a * (S + H)
+            wcol = base + S + b * P * PACK + t * P
+            nc.tensor.matmul_mx(
+                acc[:],
+                lhsT=w_dealt[b][:, a, 2 * P * t : 2 * P * (t + 1)].bitcast(FP4X4),
+                lhsT_scale=planes[:, wcol : wcol + P],
+                rhs=picked[a, c].bitcast(FP8X4),
+                rhs_scale=planes[:, base + c * BANK : base + (c + 1) * BANK],
+                start=(a == 0),
+                stop=(a == PASSES1 - 1),
+            )
+
+        th = {}
+
+        def tanh_tile(b, t, accs):
+            th[b, t] = sb([P, S], F32, "th%d_%d" % (b, t))
+            for c in range(2):
+                nc.scalar.activation(th[b, t][:, c * BANK : (c + 1) * BANK], accs[c][:], ACT.Tanh)
+
+        def stage1_tile(b, t):
+            accs = [bank(2 * t + c, "acc%d_%d_%d" % (b, t, c)) for c in range(2)]
+            for c in range(2):
+                for a in range(PASSES1):
+                    mm1(accs[c], b, t, a, c)
+            tanh_tile(b, t, accs)
+
+        def weave_dst(tile):
+            return tile[:].rearrange("p (c i t) -> p c t i", i=RUN, t=PACK)
+
+        def weave_src(tile):
+            return tile[:].rearrange("p t (c i) -> p c t i", i=RUN)
+
+        def quantize(woven, width, name):
+            codes = sb([P, width], U32, name + "_codes")
+            scales = sb([P, width], U8, name + "_scales")
+            nc.vector.quantize_mx(codes[:].bitcast(FP8X4), scales[:], woven[:])
+            return codes, scales
+
+        def gather(b, t, dst, offsets):
+            nc.vector.tensor_copy(dst[:, t, :], th[b, t][:].indirect(offsets))
+
+        def x2_abs(b, g2):
+            mags = sb([P, NP * PACK], F32, "mags%d" % b, tag="mags")
+            nc.scalar.activation(weave_dst(mags), weave_src(g2), ACT.Abs)
+            return mags
+
+        def x2_round(b, mags):
+            woven = sb([P, NP * PACK], BF16, "x2w%d" % b)
+            nc.vector.tensor_tensor(
+                woven[:].rearrange("p (n t) -> p n t", t=PACK),
+                mags[:].rearrange("p (n t) -> p n t", t=PACK),
+                weight2[:, b : b + 1, :].broadcast_to([P, NP, PACK]),
+                ALU.mult,
+            )
+            return woven
+
+        def x1_scale(b, t, g1, rounded):
+            nc.vector.tensor_scalar(rounded[:, t, :], g1[:, t, :], gain_sb[:, b, t : t + 1], None, ALU.mult)
+
+        def weave(src, width, name, tag=None):
+            woven = sb([P, width * PACK], BF16, name, tag=tag)
+            nc.scalar.copy(weave_dst(woven), weave_src(src))
+            return woven
+
+        accs0 = {(t, c): bank(2 * t + c, "acc0_%d_%d" % (t, c)) for t in range(PACK) for c in range(2)}
+        for a in range(PASSES1 - 1):
+            for t in range(PACK):
+                for c in range(2):
+                    mm1(accs0[t, c], 0, t, a, c)
+        for c in range(2):
+            for t in range(PACK):
+                mm1(accs0[t, c], 0, t, PASSES1 - 1, c)
+        w_dealt.append(deal_w(1, w_raw1))
+        row_sb = sb([P, NP], F32, "row_sb", tag="shareC")
+        nc.sync.dma_start(row_sb[:], row.partition_broadcast(P))
+
+        g2 = [sb([P, PACK, NP], F32, "g2_%d" % b) for b in range(PASSES2)]
+        g1 = sb([P, PACK, NP], F32, "g1_0")
+        r1 = sb([P, PACK, NP], BF16, "r1_0")
+        for t in range(PACK):
+            tanh_tile(0, t, [accs0[t, 0], accs0[t, 1]])
+            gather(0, t, g2[0], pos2_sb[:])
+        for t in range(PACK):
+            gather(0, t, g1, pos1_sb[:])
+            x1_scale(0, t, g1, r1)
+        for t in range(PACK):
+            stage1_tile(1, t)
+            gather(1, t, g2[1], pos2_sb[:])
+        depw = [weave(dep_raw[0], NP, "depw0", tag="th0_0")]
+        mags = x2_abs(0, g2[0])
+        x1w = weave(r1, NP, "x1w0")
+        x2q = [quantize(x2_round(0, mags), NP, "x2q0")]
+        depq = [quantize(depw[0], NP, "depq0")]
+        x1q0 = quantize(x1w, NP, "x1q0")
+        mags = x2_abs(1, g2[1])
+        depw.append(weave(dep_raw[1], NP, "depw1", tag="th0_1"))
+
+        chunks = [(0, 256), (256, 128), (384, 128)]
+        x1c = []
+        g1_last = sb([P, PACK * NP], F32, "g1_last", tag="g2_1")
+
+        def x1_chunk(i):
+            m0, width = chunks[i]
+            gc = g1_last[:, PACK * m0 : PACK * (m0 + width)].rearrange("p (t n) -> p t n", t=PACK)
+            rc = sb([P, PACK, width], BF16, "r1c%d" % i)
+            for t in range(PACK):
+                gather(1, t, gc, pos1_sb[:, m0 // 16 : (m0 + width) // 16])
+            for t in range(PACK):
+                x1_scale(1, t, gc, rc)
+            x1c.append(weave(rc, width, "x1wc%d" % i))
+
+        x1_chunk(0)
+        x2q.append(quantize(x2_round(1, mags), NP, "x2q1"))
+        x1_chunk(1)
+        x1_chunk(2)
+        depq.append(quantize(depw[1], NP, "depq1"))
+
+        def mm2(acc, lhs, m0, rhs, start, stop):
+            nc.tensor.matmul_mx(
+                acc[:],
+                lhsT=lhs[0][:, m0 : m0 + P].bitcast(FP8X4),
+                lhsT_scale=lhs[1][:, m0 : m0 + P],
+                rhs=rhs[0][:].bitcast(FP8X4),
+                rhs_scale=rhs[1][:],
+                start=start,
+                stop=stop,
+            )
+
+        scores = [bank(i, "score%d" % i) for i in range(NP // P)]
+        for i in range(NP // P):
+            mm2(scores[i], x1q0, i * P, x2q[0], True, False)
+        for b in range(PASSES2):
+            for i in range(NP // P):
+                mm2(scores[i], depq[b], i * P, x2q[b], False, False)
+        for ci, (m0, width) in enumerate(chunks):
+            x1q = quantize(x1c[ci], width, "x1qc%d" % ci)
+            for i in range(m0 // P, (m0 + width) // P):
+                mm2(scores[i], x1q, i * P - m0, x2q[1], False, True)
+                te = sb([P, NP], F32, "te%d" % i)
+                nc.scalar.activation(te[:], scores[i][:], ACT.Tanh)
+                res = sb([P, NP], F32, "res%d" % i)
+                nc.vector.scalar_tensor_tensor(res[:], te[:], col_sb[:, i : i + 1], row_sb[:], ALU.mult, ALU.add)
+                nc.sync.dma_start(out[i * P : (i + 1) * P, :], res[:])

@@ -22,8 +22,12 @@ PASSES1 = K // (P * PACK)
 PASSES2 = H // (P * PACK)
 BANK = 512
 SCALE_ROWS = 16
-ROW0 = 40
+ROW0 = 36
+ROW1 = ROW0 + 2 * SCALE_ROWS
 RUN = 4
+TAB_BYTES = 4 * T
+PICKED0_AT = 3 * TAB_BYTES
+TAB_SC_AT = PICKED0_AT + 4 * S
 
 
 def tile_list_claim_chart_scores_kernel(
@@ -33,10 +37,14 @@ def tile_list_claim_chart_scores_kernel(
     with ExitStack() as ctx:
         lists = ctx.enter_context(tc.tile_pool(name="lists", bufs=1))
         keep = ctx.enter_context(tc.tile_pool(name="keep", bufs=1))
+        laid = ctx.enter_context(tc.tile_pool(name="laid", bufs=1))
         psum = ctx.enter_context(tc.psum_pool(name="psum", bufs=1))
 
         def sb(shape, dtype, name, tag=None):
             return keep.tile(shape, dtype, name=name, tag=tag or name, align_bytes=64)
+
+        def at(offset, shape, dtype, name):
+            return laid.tile(shape, dtype, name=name, offset=offset, align_bytes=64)
 
         def bank(i, name):
             return psum.tile([P, BANK], F32, name=name, tag="bank%d" % i)
@@ -48,74 +56,64 @@ def tile_list_claim_chart_scores_kernel(
         nc.sync.dma_start(pos1_sb[:], pos1)
         nc.sync.dma_start(pos2_sb[:], pos2)
 
-        n_rows = SCALE_ROWS * PASSES1
-        tab_sc = sb([P, T], U8, "tab_sc")
-        nc.vector.memset(tab_sc[:].bitcast(I32), 0)
-        nc.scalar.dma_start(
-            tab_sc[ROW0 : ROW0 + n_rows, :].bitcast(I32), tab_scales.rearrange("a q t -> q a t").bitcast(I32)
-        )
-        w_sc = sb([P, H], U8, "w_sc", tag="shareD")
-        nc.vector.memset(w_sc[:].bitcast(I32), 0)
-        nc.scalar.dma_start(
-            w_sc[ROW0 : ROW0 + n_rows, :].bitcast(I32), w4_scales.rearrange("a q c -> q a c").bitcast(I32)
-        )
+        def load_scale_rows(tile, rows):
+            nc.vector.memset(tile[:].bitcast(I32), 0)
+            nc.scalar.dma_start(
+                tile[ROW0:ROW1, :].bitcast(I32), rows[0:2].rearrange("a q n -> q a n").bitcast(I32)
+            )
+            nc.scalar.dma_start(tile[ROW1 : ROW1 + SCALE_ROWS, :].bitcast(I32), rows[2].bitcast(I32))
+
+        tab_sc = at(TAB_SC_AT, [P, T], U8, "tab_sc")
+        load_scale_rows(tab_sc, tab_scales)
+        w_sc = at(TAB_BYTES, [P, H], U8, "w_sc")
+        load_scale_rows(w_sc, w4_scales)
         planes = sb([P, PASSES1 * (S + H)], U8, "planes")
         nc.vector.memset(planes[:].bitcast(I32), 0)
 
-        half = 2 * P * PACK
+        w_raw = sb([P, PASSES1, 2 * H], U8, "w_raw")
+        nc.sync.dma_start(w_raw[:].bitcast(I32), w4_words.rearrange("a p c -> p a c").bitcast(I32))
 
-        def load_w(b, tag):
-            raw = sb([P, PASSES1, half], U8, "w_raw%d" % b, tag=tag)
-            nc.sync.dma_start(
-                raw[:].bitcast(I32),
-                w4_words.rearrange("a p c -> p a c")[:, :, b * half : (b + 1) * half].bitcast(I32),
-            )
-            return raw
-
-        def deal_w(b, raw):
-            dealt = sb([P, PASSES1, half], U8, "w_dealt%d" % b)
-            for a in range(PASSES1):
-                nc.vector.tensor_copy(
-                    dealt[:, a, :].bitcast(U16).rearrange("p (t q) -> p t q", t=PACK),
-                    raw[:, a, :].bitcast(U16).rearrange("p (q t) -> p t q", t=PACK),
-                )
-            return dealt
-
-        def load_tab(a, tag):
-            words = sb([P, T], I32, "tab%d" % a, tag=tag)
+        def load_tab(a):
+            words = at(a * TAB_BYTES, [P, T], I32, "tab%d" % a)
             nc.sync.dma_start(words[:], tab_words[a].rearrange("p t i -> p (t i)").bitcast(I32))
             return words
 
-        w_raw0 = load_w(0, "shareB")
-        tabs = [load_tab(0, "tab0")]
+        tabs = [load_tab(0)]
 
         gain_sb = sb([P, PASSES2, PACK], F32, "gain_sb")
         disc_sb = sb([P, PASSES2, PACK], F32, "disc_sb")
-        col_sb = sb([P, NP // P], F32, "col_sb")
         nc.gpsimd.dma_start(gain_sb[:], gain.rearrange("(b p t) -> p b t", p=P, t=PACK))
         nc.gpsimd.dma_start(disc_sb[:], disc.rearrange("(b p t) -> p b t", p=P, t=PACK))
-        with nc.allow_non_contiguous_dma(reason="one value of col to a partition"):
-            nc.gpsimd.dma_start(col_sb[:], col.rearrange("(i p) -> p i", p=P))
 
-        w_dealt = [deal_w(0, w_raw0)]
-        tabs.append(load_tab(1, "shareB"))
+        def deal_w(a, dealt):
+            nc.vector.tensor_copy(
+                dealt[:].bitcast(U16).rearrange("p (b t q) -> p b t q", b=PASSES2, t=PACK),
+                w_raw[:, a, :].bitcast(U16).rearrange("p (b q t) -> p b t q", b=PASSES2, t=PACK),
+            )
+            return dealt
 
-        picked_sc = sb([P, S], U8, "picked_sc")
-        nc.vector.tensor_copy(picked_sc[:], tab_sc[:].indirect(offs_sb[:]))
-        stage = sb([P, S + H], U8, "stage", tag="shareC")
-        nc.vector.tensor_copy(stage[:, :S].bitcast(I32), picked_sc[:].bitcast(I32))
+        stage = sb([P, S + H], U8, "stage")
         nc.vector.tensor_copy(
             stage[:, S:].rearrange("p (b t q) -> p b t q", b=PASSES2, t=PACK),
             w_sc[:].rearrange("p (b q t) -> p b t q", b=PASSES2, t=PACK),
         )
+        tabs.append(load_tab(1))
+        picked_sc = at(PICKED0_AT - S // 2, [P, S], U8, "picked_sc")
+        nc.vector.tensor_copy(picked_sc[:], tab_sc[:].indirect(offs_sb[:]))
+        nc.vector.tensor_copy(stage[:, :S].bitcast(I32), picked_sc[:].bitcast(I32))
+        w_dealt = [deal_w(0, sb([P, 2 * H], U8, "w_dealt0"))]
+        pair = 2 * (S + H)
         for quad in range(4):
-            src0 = ROW0 + 4 * PASSES1 * quad
-            nc.sync.dma_start(
-                planes[32 * quad : 32 * quad + 4, :].bitcast(I32).rearrange("r (a n) -> r a n", a=PASSES1),
-                stage[src0 : src0 + 4 * PASSES1, :].bitcast(I32),
+            nc.scalar.dma_start(
+                planes[32 * quad : 32 * quad + 4, :pair].bitcast(I32).rearrange("r (a n) -> r a n", a=2),
+                stage[ROW0 + 8 * quad : ROW0 + 8 * (quad + 1), :].bitcast(I32),
             )
-        tabs.append(load_tab(2, "shareD"))
-        w_raw1 = load_w(1, "shareC")
+        tabs.append(load_tab(2))
+        for quad in range(4):
+            nc.scalar.dma_start(
+                planes[32 * quad : 32 * quad + 4, pair:].bitcast(I32),
+                stage[ROW1 + 4 * quad : ROW1 + 4 * (quad + 1), :].bitcast(I32),
+            )
 
         mag = sb([P, PASSES2 * PACK], F32, "mag")
         gain_flat = gain_sb[:].rearrange("p b t -> p (b t)")
@@ -127,14 +125,25 @@ def tile_list_claim_chart_scores_kernel(
             weight2[:].rearrange("p b t -> p (b t)"), mag[:], disc_sb[:].rearrange("p b t -> p (b t)"), ALU.mult
         )
 
+        def gain_rows(b):
+            return gain_sb[:, b, :].unsqueeze(2).broadcast_to([P, PACK, NP])
+
         picked = {}
+        gain_wide = []
         for a in range(PASSES1):
             window = tabs[a][:].bitcast(U32)
             if a < PASSES1 - 1:
-                g = sb([P, S], U32, "picked%d" % a)
+                g = at(PICKED0_AT, [P, S], U32, "picked0") if a == 0 else sb([P, S], U32, "picked%d" % a)
                 nc.vector.tensor_copy(g[:], window.indirect(offs_sb[:]))
                 for c in range(2):
                     picked[a, c] = g[:, c * BANK : (c + 1) * BANK]
+                w_dealt.append(deal_w(a + 1, at(TAB_SC_AT + 2 * H * a, [P, 2 * H], U8, "w_dealt%d" % (a + 1))))
+                if a == 0:
+                    gain_wide.append(at(0, [P, PACK, NP], F32, "gain_wide0"))
+                    nc.scalar.copy(gain_wide[0][:], gain_rows(0))
+                else:
+                    gain_wide.append(at(TAB_BYTES + TAB_BYTES // 2, [P, PACK, NP], F32, "gain_wide1"))
+                    nc.vector.tensor_copy(gain_wide[1][:], gain_rows(1))
             else:
                 for c in range(2):
                     g = sb([P, BANK], U32, "picked%d_%d" % (a, c))
@@ -142,17 +151,18 @@ def tile_list_claim_chart_scores_kernel(
                     picked[a, c] = g[:]
 
         dep_raw = []
-        for b, tag in enumerate(("shareB", "shareD")):
-            raw = sb([P, PACK, NP], F32, "dep_raw%d" % b, tag=tag)
+        for b in range(PASSES2):
+            raw = at((b + 1) * TAB_BYTES, [P, PACK, NP], F32, "dep_raw%d" % b)
             nc.sync.dma_start(raw[:], dep[b * P * PACK : (b + 1) * P * PACK, :].rearrange("(p t) m -> p t m", t=PACK))
             dep_raw.append(raw)
 
         def mm1(acc, b, t, a, c):
             base = a * (S + H)
-            wcol = base + S + b * P * PACK + t * P
+            wtile = b * P * PACK + t * P
+            wcol = base + S + wtile
             nc.tensor.matmul_mx(
                 acc[:],
-                lhsT=w_dealt[b][:, a, 2 * P * t : 2 * P * (t + 1)].bitcast(FP4X4),
+                lhsT=w_dealt[a][:, 2 * wtile : 2 * (wtile + P)].bitcast(FP4X4),
                 lhsT_scale=planes[:, wcol : wcol + P],
                 rhs=picked[a, c].bitcast(FP8X4),
                 rhs_scale=planes[:, base + c * BANK : base + (c + 1) * BANK],
@@ -204,8 +214,10 @@ def tile_list_claim_chart_scores_kernel(
             )
             return woven
 
-        def x1_scale(b, t, g1, rounded):
-            nc.vector.tensor_scalar(rounded[:, t, :], g1[:, t, :], gain_sb[:, b, t : t + 1], None, ALU.mult)
+        def gather_gain(b, t, dst, offsets, width):
+            nc.vector.tensor_tensor(
+                dst[:, t, :], th[b, t][:].indirect(offsets), gain_wide[b][:, t, :width], ALU.mult
+            )
 
         def weave(src, width, name, tag=None):
             woven = sb([P, width * PACK], BF16, name, tag=tag)
@@ -220,25 +232,25 @@ def tile_list_claim_chart_scores_kernel(
         for c in range(2):
             for t in range(PACK):
                 mm1(accs0[t, c], 0, t, PASSES1 - 1, c)
-        w_dealt.append(deal_w(1, w_raw1))
-        row_sb = sb([P, NP], F32, "row_sb", tag="shareC")
+        row_sb = at(2 * TAB_BYTES + TAB_BYTES // 2, [P, NP], F32, "row_sb")
         nc.sync.dma_start(row_sb[:], row.partition_broadcast(P))
+        col_sb = at(2 * TAB_BYTES + TAB_BYTES // 2 + 4 * NP, [P, NP // P], F32, "col_sb")
+        with nc.allow_non_contiguous_dma(reason="one value of col to a partition"):
+            nc.sync.dma_start(col_sb[:], col.rearrange("(i p) -> p i", p=P))
 
         g2 = [sb([P, PACK, NP], F32, "g2_%d" % b) for b in range(PASSES2)]
         g1 = sb([P, PACK, NP], F32, "g1_0")
-        r1 = sb([P, PACK, NP], BF16, "r1_0")
         for t in range(PACK):
             tanh_tile(0, t, [accs0[t, 0], accs0[t, 1]])
             gather(0, t, g2[0], pos2_sb[:])
         for t in range(PACK):
-            gather(0, t, g1, pos1_sb[:])
-            x1_scale(0, t, g1, r1)
+            gather_gain(0, t, g1, pos1_sb[:], NP)
         for t in range(PACK):
             stage1_tile(1, t)
             gather(1, t, g2[1], pos2_sb[:])
         depw = [weave(dep_raw[0], NP, "depw0", tag="th0_0")]
         mags = x2_abs(0, g2[0])
-        x1w = weave(r1, NP, "x1w0")
+        x1w = weave(g1, NP, "x1w0")
         x2q = [quantize(x2_round(0, mags), NP, "x2q0")]
         depq = [quantize(depw[0], NP, "depq0")]
         x1q0 = quantize(x1w, NP, "x1q0")
@@ -252,18 +264,15 @@ def tile_list_claim_chart_scores_kernel(
         def x1_chunk(i):
             m0, width = chunks[i]
             gc = g1_last[:, PACK * m0 : PACK * (m0 + width)].rearrange("p (t n) -> p t n", t=PACK)
-            rc = sb([P, PACK, width], BF16, "r1c%d" % i)
             for t in range(PACK):
-                gather(1, t, gc, pos1_sb[:, m0 // 16 : (m0 + width) // 16])
-            for t in range(PACK):
-                x1_scale(1, t, gc, rc)
-            x1c.append(weave(rc, width, "x1wc%d" % i))
+                gather_gain(1, t, gc, pos1_sb[:, m0 // 16 : (m0 + width) // 16], width)
+            x1c.append(weave(gc, width, "x1wc%d" % i))
 
         x1_chunk(0)
         x2q.append(quantize(x2_round(1, mags), NP, "x2q1"))
+        depq.append(quantize(depw[1], NP, "depq1"))
         x1_chunk(1)
         x1_chunk(2)
-        depq.append(quantize(depw[1], NP, "depq1"))
 
         def mm2(acc, lhs, m0, rhs, start, stop):
             nc.tensor.matmul_mx(

@@ -25,6 +25,7 @@ SCALE_ROWS = 16
 ROW0 = 36
 ROW1 = ROW0 + 2 * SCALE_ROWS
 RUN = 4
+PAIRS = 3
 TAB_BYTES = 4 * T
 PICKED0_AT = 3 * TAB_BYTES
 TAB_SC_AT = PICKED0_AT + 4 * S
@@ -53,32 +54,32 @@ def tile_list_claim_chart_scores_kernel(
         pos1_sb = lists.tile([P, NP // 16], U16, name="pos1_sb")
         pos2_sb = lists.tile([P, NP // 16], U16, name="pos2_sb")
         nc.sync.dma_start(offs_sb[:], offs)
+        w_raw = sb([P, PASSES1, 2 * H], U8, "w_raw")
+        nc.sync.dma_start(w_raw[:].bitcast(I32), w4_words.rearrange("a p c -> p a c").bitcast(I32))
         nc.sync.dma_start(pos1_sb[:], pos1)
         nc.sync.dma_start(pos2_sb[:], pos2)
 
         def load_scale_rows(tile, rows):
             nc.vector.memset(tile[:].bitcast(I32), 0)
-            nc.scalar.dma_start(
+            nc.sync.dma_start(
                 tile[ROW0:ROW1, :].bitcast(I32), rows[0:2].rearrange("a q n -> q a n").bitcast(I32)
             )
-            nc.scalar.dma_start(tile[ROW1 : ROW1 + SCALE_ROWS, :].bitcast(I32), rows[2].bitcast(I32))
+            nc.sync.dma_start(tile[ROW1 : ROW1 + SCALE_ROWS, :].bitcast(I32), rows[2].bitcast(I32))
 
         tab_sc = at(TAB_SC_AT, [P, T], U8, "tab_sc")
         load_scale_rows(tab_sc, tab_scales)
-        w_sc = at(TAB_BYTES, [P, H], U8, "w_sc")
+        w_sc = at(2 * TAB_BYTES, [P, H], U8, "w_sc")
         load_scale_rows(w_sc, w4_scales)
         planes = sb([P, PASSES1 * (S + H)], U8, "planes")
         nc.vector.memset(planes[:].bitcast(I32), 0)
 
-        w_raw = sb([P, PASSES1, 2 * H], U8, "w_raw")
-        nc.sync.dma_start(w_raw[:].bitcast(I32), w4_words.rearrange("a p c -> p a c").bitcast(I32))
 
         def load_tab(a):
             words = at(a * TAB_BYTES, [P, T], I32, "tab%d" % a)
             nc.sync.dma_start(words[:], tab_words[a].rearrange("p t i -> p (t i)").bitcast(I32))
             return words
 
-        tabs = [load_tab(0)]
+        tabs = [load_tab(0), load_tab(1)]
 
         gain_sb = sb([P, PASSES2, PACK], F32, "gain_sb")
         disc_sb = sb([P, PASSES2, PACK], F32, "disc_sb")
@@ -92,25 +93,24 @@ def tile_list_claim_chart_scores_kernel(
             )
             return dealt
 
+        picked_sc = at(PICKED0_AT - S // 2, [P, S], U8, "picked_sc")
+        nc.vector.tensor_copy(picked_sc[:], tab_sc[:].indirect(offs_sb[:]))
         stage = sb([P, S + H], U8, "stage")
         nc.vector.tensor_copy(
             stage[:, S:].rearrange("p (b t q) -> p b t q", b=PASSES2, t=PACK),
             w_sc[:].rearrange("p (b q t) -> p b t q", b=PASSES2, t=PACK),
         )
-        tabs.append(load_tab(1))
-        picked_sc = at(PICKED0_AT - S // 2, [P, S], U8, "picked_sc")
-        nc.vector.tensor_copy(picked_sc[:], tab_sc[:].indirect(offs_sb[:]))
         nc.vector.tensor_copy(stage[:, :S].bitcast(I32), picked_sc[:].bitcast(I32))
         w_dealt = [deal_w(0, sb([P, 2 * H], U8, "w_dealt0"))]
         pair = 2 * (S + H)
         for quad in range(4):
-            nc.scalar.dma_start(
+            nc.sync.dma_start(
                 planes[32 * quad : 32 * quad + 4, :pair].bitcast(I32).rearrange("r (a n) -> r a n", a=2),
                 stage[ROW0 + 8 * quad : ROW0 + 8 * (quad + 1), :].bitcast(I32),
             )
         tabs.append(load_tab(2))
         for quad in range(4):
-            nc.scalar.dma_start(
+            nc.sync.dma_start(
                 planes[32 * quad : 32 * quad + 4, pair:].bitcast(I32),
                 stage[ROW1 + 4 * quad : ROW1 + 4 * (quad + 1), :].bitcast(I32),
             )
@@ -138,12 +138,8 @@ def tile_list_claim_chart_scores_kernel(
                 for c in range(2):
                     picked[a, c] = g[:, c * BANK : (c + 1) * BANK]
                 w_dealt.append(deal_w(a + 1, at(TAB_SC_AT + 2 * H * a, [P, 2 * H], U8, "w_dealt%d" % (a + 1))))
-                if a == 0:
-                    gain_wide.append(at(0, [P, PACK, NP], F32, "gain_wide0"))
-                    nc.scalar.copy(gain_wide[0][:], gain_rows(0))
-                else:
-                    gain_wide.append(at(TAB_BYTES + TAB_BYTES // 2, [P, PACK, NP], F32, "gain_wide1"))
-                    nc.vector.tensor_copy(gain_wide[1][:], gain_rows(1))
+                gain_wide.append(sb([P, PACK, NP], F32, "gain_wide%d" % a))
+                nc.scalar.copy(gain_wide[a][:], gain_rows(a))
             else:
                 for c in range(2):
                     g = sb([P, BANK], U32, "picked%d_%d" % (a, c))
@@ -178,7 +174,7 @@ def tile_list_claim_chart_scores_kernel(
                 nc.scalar.activation(th[b, t][:, c * BANK : (c + 1) * BANK], accs[c][:], ACT.Tanh)
 
         def stage1_tile(b, t):
-            accs = [bank(2 * t + c, "acc%d_%d_%d" % (b, t, c)) for c in range(2)]
+            accs = [bank(2 * ((PACK * b + t) % PAIRS) + c, "acc%d_%d_%d" % (b, t, c)) for c in range(2)]
             for c in range(2):
                 for a in range(PASSES1):
                     mm1(accs[c], b, t, a, c)
@@ -224,13 +220,13 @@ def tile_list_claim_chart_scores_kernel(
             nc.scalar.copy(weave_dst(woven), weave_src(src))
             return woven
 
-        accs0 = {(t, c): bank(2 * t + c, "acc0_%d_%d" % (t, c)) for t in range(PACK) for c in range(2)}
+        accs0 = {(t, c): bank(2 * t + c, "acc0_%d_%d" % (t, c)) for t in range(PAIRS) for c in range(2)}
         for a in range(PASSES1 - 1):
-            for t in range(PACK):
+            for t in range(PAIRS):
                 for c in range(2):
                     mm1(accs0[t, c], 0, t, a, c)
         for c in range(2):
-            for t in range(PACK):
+            for t in range(PAIRS):
                 mm1(accs0[t, c], 0, t, PASSES1 - 1, c)
         row_sb = at(2 * TAB_BYTES + TAB_BYTES // 2, [P, NP], F32, "row_sb")
         nc.sync.dma_start(row_sb[:], row.partition_broadcast(P))
@@ -241,7 +237,10 @@ def tile_list_claim_chart_scores_kernel(
         g2 = [sb([P, PACK, NP], F32, "g2_%d" % b) for b in range(PASSES2)]
         g1 = sb([P, PACK, NP], F32, "g1_0")
         for t in range(PACK):
-            tanh_tile(0, t, [accs0[t, 0], accs0[t, 1]])
+            if t < PAIRS:
+                tanh_tile(0, t, [accs0[t, 0], accs0[t, 1]])
+            else:
+                stage1_tile(0, t)
             gather(0, t, g2[0], pos2_sb[:])
         for t in range(PACK):
             gather_gain(0, t, g1, pos1_sb[:], NP)
@@ -285,7 +284,7 @@ def tile_list_claim_chart_scores_kernel(
                 stop=stop,
             )
 
-        scores = [bank(i, "score%d" % i) for i in range(NP // P)]
+        scores = [bank((2 * PAIRS + i) % 8, "score%d" % i) for i in range(NP // P)]
         for i in range(NP // P):
             mm2(scores[i], x1q0, i * P, x2q[0], True, False)
         for b in range(PASSES2):

@@ -29,6 +29,7 @@ PAIRS = 3
 TAB_BYTES = 4 * T
 PICKED0_AT = 3 * TAB_BYTES
 TAB_SC_AT = PICKED0_AT + 4 * S
+W_RAW_AT = TAB_SC_AT + T
 
 
 def tile_list_claim_chart_scores_kernel(
@@ -54,7 +55,7 @@ def tile_list_claim_chart_scores_kernel(
         pos1_sb = lists.tile([P, NP // 16], U16, name="pos1_sb")
         pos2_sb = lists.tile([P, NP // 16], U16, name="pos2_sb")
         nc.sync.dma_start(offs_sb[:], offs)
-        w_raw = sb([P, PASSES1, 2 * H], U8, "w_raw")
+        w_raw = at(W_RAW_AT, [P, PASSES1, 2 * H], U8, "w_raw")
         nc.sync.dma_start(w_raw[:].bitcast(I32), w4_words.rearrange("a p c -> p a c").bitcast(I32))
         nc.sync.dma_start(pos1_sb[:], pos1)
         nc.sync.dma_start(pos2_sb[:], pos2)
@@ -81,11 +82,6 @@ def tile_list_claim_chart_scores_kernel(
 
         tabs = [load_tab(0), load_tab(1)]
 
-        gain_sb = sb([P, PASSES2, PACK], F32, "gain_sb")
-        disc_sb = sb([P, PASSES2, PACK], F32, "disc_sb")
-        nc.gpsimd.dma_start(gain_sb[:], gain.rearrange("(b p t) -> p b t", p=P, t=PACK))
-        nc.gpsimd.dma_start(disc_sb[:], disc.rearrange("(b p t) -> p b t", p=P, t=PACK))
-
         def deal_w(a, dealt):
             nc.vector.tensor_copy(
                 dealt[:].bitcast(U16).rearrange("p (b t q) -> p b t q", b=PASSES2, t=PACK),
@@ -103,33 +99,19 @@ def tile_list_claim_chart_scores_kernel(
         nc.vector.tensor_copy(stage[:, :S].bitcast(I32), picked_sc[:].bitcast(I32))
         w_dealt = [deal_w(0, sb([P, 2 * H], U8, "w_dealt0"))]
         pair = 2 * (S + H)
-        for quad in range(4):
+        for quad in (0, 2, 1, 3):
             nc.sync.dma_start(
                 planes[32 * quad : 32 * quad + 4, :pair].bitcast(I32).rearrange("r (a n) -> r a n", a=2),
                 stage[ROW0 + 8 * quad : ROW0 + 8 * (quad + 1), :].bitcast(I32),
             )
         tabs.append(load_tab(2))
-        for quad in range(4):
+        for quad in (0, 2, 1, 3):
             nc.sync.dma_start(
                 planes[32 * quad : 32 * quad + 4, pair:].bitcast(I32),
                 stage[ROW1 + 4 * quad : ROW1 + 4 * (quad + 1), :].bitcast(I32),
             )
 
-        mag = sb([P, PASSES2 * PACK], F32, "mag")
-        gain_flat = gain_sb[:].rearrange("p b t -> p (b t)")
-        twice = sb([P, PASSES2 * PACK], F32, "twice")
-        nc.gpsimd.tensor_scalar(twice[:], gain_flat, 0.0, 2.0, ALU.max, ALU.mult)
-        nc.gpsimd.tensor_tensor(mag[:], twice[:], gain_flat, ALU.subtract)
-        weight2 = sb([P, PASSES2, PACK], F32, "weight2")
-        nc.gpsimd.tensor_tensor(
-            weight2[:].rearrange("p b t -> p (b t)"), mag[:], disc_sb[:].rearrange("p b t -> p (b t)"), ALU.mult
-        )
-
-        def gain_rows(b):
-            return gain_sb[:, b, :].unsqueeze(2).broadcast_to([P, PACK, NP])
-
         picked = {}
-        gain_wide = []
         for a in range(PASSES1):
             window = tabs[a][:].bitcast(U32)
             if a < PASSES1 - 1:
@@ -138,17 +120,33 @@ def tile_list_claim_chart_scores_kernel(
                 for c in range(2):
                     picked[a, c] = g[:, c * BANK : (c + 1) * BANK]
                 w_dealt.append(deal_w(a + 1, at(TAB_SC_AT + 2 * H * a, [P, 2 * H], U8, "w_dealt%d" % (a + 1))))
-                gain_wide.append(sb([P, PACK, NP], F32, "gain_wide%d" % a))
-                nc.scalar.copy(gain_wide[a][:], gain_rows(a))
             else:
                 for c in range(2):
                     g = sb([P, BANK], U32, "picked%d_%d" % (a, c))
                     nc.vector.tensor_copy(g[:], window.indirect(offs_sb[:, c * 32 : (c + 1) * 32]))
                     picked[a, c] = g[:]
 
+        gain_sb = at(W_RAW_AT, [P, PASSES2, PACK], F32, "gain_sb")
+        disc_sb = at(W_RAW_AT + 64, [P, PASSES2, PACK], F32, "disc_sb")
+        nc.sync.dma_start(gain_sb[:], gain.rearrange("(b p t) -> p b t", p=P, t=PACK))
+        nc.sync.dma_start(disc_sb[:], disc.rearrange("(b p t) -> p b t", p=P, t=PACK))
+
+        def gain_rows(b, width):
+            return gain_sb[:, b, :].unsqueeze(2).broadcast_to([P, PACK, width])
+
+        gain_wide = [sb([P, PACK, NP], F32, "gain_wide0"), sb([P, PACK, NP // 2], F32, "gain_wide1")]
+        nc.vector.tensor_copy(gain_wide[0][:], gain_rows(0, NP))
+        mag = sb([P, PASSES2 * PACK], F32, "mag")
+        gain_flat = gain_sb[:].rearrange("p b t -> p (b t)")
+        nc.vector.scalar_tensor_tensor(mag[:], gain_flat, -1.0, gain_flat, ALU.mult, ALU.max)
+        weight2 = sb([P, PASSES2, PACK], F32, "weight2")
+        nc.vector.tensor_tensor(
+            weight2[:].rearrange("p b t -> p (b t)"), mag[:], disc_sb[:].rearrange("p b t -> p (b t)"), ALU.mult
+        )
+
         dep_raw = []
         for b in range(PASSES2):
-            raw = at((b + 1) * TAB_BYTES, [P, PACK, NP], F32, "dep_raw%d" % b)
+            raw = at(W_RAW_AT + 128 if b == 0 else 2 * TAB_BYTES, [P, PACK, NP], F32, "dep_raw%d" % b)
             nc.sync.dma_start(raw[:], dep[b * P * PACK : (b + 1) * P * PACK, :].rearrange("(p t) m -> p t m", t=PACK))
             dep_raw.append(raw)
 
@@ -248,54 +246,69 @@ def tile_list_claim_chart_scores_kernel(
             stage1_tile(1, t)
             gather(1, t, g2[1], pos2_sb[:])
         depw = [weave(dep_raw[0], NP, "depw0", tag="th0_0")]
-        mags = x2_abs(0, g2[0])
+        mags0 = sb([P, PACK, NP], F32, "mags0")
+        nc.scalar.activation(mags0[:], g2[0][:], ACT.Abs)
         x1w = weave(g1, NP, "x1w0")
-        x2q = [quantize(x2_round(0, mags), NP, "x2q0")]
+        rounded = sb([P, PACK, NP], BF16, "rounded")
+        for t in range(PACK):
+            nc.vector.tensor_scalar(rounded[:, t, :], mags0[:, t, :], weight2[:, 0, t : t + 1], None, ALU.mult)
         depq = [quantize(depw[0], NP, "depq0")]
         x1q0 = quantize(x1w, NP, "x1q0")
+        nc.scalar.copy(gain_wide[1][:], gain_rows(1, NP // 2))
+        x2w0 = weave(rounded, NP, "x2w0")
         mags = x2_abs(1, g2[1])
         depw.append(weave(dep_raw[1], NP, "depw1", tag="th0_1"))
 
-        chunks = [(0, 256), (256, 128), (384, 128)]
+        chunks = [(0, 256, "mags0"), (256, 128, "x2w0"), (384, 128, "x2w1")]
         x1c = []
-        g1_last = sb([P, PACK * NP], F32, "g1_last", tag="g2_1")
 
         def x1_chunk(i):
-            m0, width = chunks[i]
-            gc = g1_last[:, PACK * m0 : PACK * (m0 + width)].rearrange("p (t n) -> p t n", t=PACK)
+            m0, width, tag = chunks[i]
+            gc = sb([P, PACK, width], F32, "g1c%d" % i, tag=tag)
             for t in range(PACK):
                 gather_gain(1, t, gc, pos1_sb[:, m0 // 16 : (m0 + width) // 16], width)
             x1c.append(weave(gc, width, "x1wc%d" % i))
 
         x1_chunk(0)
+        x2q = [quantize(x2w0, NP, "x2q0")]
+        x1_chunk(1)
         x2q.append(quantize(x2_round(1, mags), NP, "x2q1"))
         depq.append(quantize(depw[1], NP, "depq1"))
-        x1_chunk(1)
-        x1_chunk(2)
 
-        def mm2(acc, lhs, m0, rhs, start, stop):
+        parts = [(i, 0, NP) for i in range(NP // P - 1)] + [(NP // P - 1, j0, NP // 2) for j0 in (0, NP // 2)]
+        scores = [
+            psum.tile([P, width], F32, name="score%d" % n, tag="bank%d" % ((2 * PAIRS + n) % 8))
+            for n, (i, j0, width) in enumerate(parts)
+        ]
+
+        def mm2(n, lhs, m0, rhs, start, stop):
+            i, j0, width = parts[n]
             nc.tensor.matmul_mx(
-                acc[:],
-                lhsT=lhs[0][:, m0 : m0 + P].bitcast(FP8X4),
-                lhsT_scale=lhs[1][:, m0 : m0 + P],
-                rhs=rhs[0][:].bitcast(FP8X4),
-                rhs_scale=rhs[1][:],
+                scores[n][:],
+                lhsT=lhs[0][:, i * P - m0 : (i + 1) * P - m0].bitcast(FP8X4),
+                lhsT_scale=lhs[1][:, i * P - m0 : (i + 1) * P - m0],
+                rhs=rhs[0][:, j0 : j0 + width].bitcast(FP8X4),
+                rhs_scale=rhs[1][:, j0 : j0 + width],
                 start=start,
                 stop=stop,
             )
 
-        scores = [bank((2 * PAIRS + i) % 8, "score%d" % i) for i in range(NP // P)]
-        for i in range(NP // P):
-            mm2(scores[i], x1q0, i * P, x2q[0], True, False)
+        for n in range(len(parts)):
+            mm2(n, x1q0, 0, x2q[0], True, False)
         for b in range(PASSES2):
-            for i in range(NP // P):
-                mm2(scores[i], depq[b], i * P, x2q[b], False, False)
-        for ci, (m0, width) in enumerate(chunks):
-            x1q = quantize(x1c[ci], width, "x1qc%d" % ci)
-            for i in range(m0 // P, (m0 + width) // P):
-                mm2(scores[i], x1q, i * P - m0, x2q[1], False, True)
-                te = sb([P, NP], F32, "te%d" % i)
-                nc.scalar.activation(te[:], scores[i][:], ACT.Tanh)
-                res = sb([P, NP], F32, "res%d" % i)
-                nc.vector.scalar_tensor_tensor(res[:], te[:], col_sb[:, i : i + 1], row_sb[:], ALU.mult, ALU.add)
-                nc.sync.dma_start(out[i * P : (i + 1) * P, :], res[:])
+            for n in range(len(parts)):
+                mm2(n, depq[b], 0, x2q[b], False, False)
+        for ci, (m0, count, tag) in enumerate(chunks):
+            if ci == 1:
+                x1_chunk(2)
+            x1q = quantize(x1c[ci], count, "x1qc%d" % ci)
+            for n, (i, j0, width) in enumerate(parts):
+                if m0 <= i * P < m0 + count:
+                    mm2(n, x1q, m0, x2q[1], False, True)
+                    te = sb([P, width], F32, "te%d" % n)
+                    nc.scalar.activation(te[:], scores[n][:], ACT.Tanh)
+                    res = sb([P, width], F32, "res%d" % n)
+                    nc.vector.scalar_tensor_tensor(
+                        res[:], te[:], col_sb[:, i : i + 1], row_sb[:, j0 : j0 + width], ALU.mult, ALU.add
+                    )
+                    nc.sync.dma_start(out[i * P : (i + 1) * P, j0 : j0 + width], res[:])

@@ -28,8 +28,9 @@ RUN = 4
 PAIRS = 3
 TAB_BYTES = 4 * T
 PICKED0_AT = 3 * TAB_BYTES
-TAB_SC_AT = PICKED0_AT + 4 * S
-W_RAW_AT = TAB_SC_AT + T
+DEALT_AT = PICKED0_AT + 4 * S
+TAB_SC_AT = DEALT_AT + H
+W_RAW_AT = DEALT_AT + PASSES1 * 2 * H
 
 
 def tile_list_claim_chart_scores_kernel(
@@ -97,7 +98,7 @@ def tile_list_claim_chart_scores_kernel(
             w_sc[:].rearrange("p (b q t) -> p b t q", b=PASSES2, t=PACK),
         )
         nc.vector.tensor_copy(stage[:, :S].bitcast(I32), picked_sc[:].bitcast(I32))
-        w_dealt = [deal_w(0, sb([P, 2 * H], U8, "w_dealt0"))]
+        w_dealt = [deal_w(0, at(DEALT_AT, [P, 2 * H], U8, "w_dealt0"))]
         pair = 2 * (S + H)
         for quad in (0, 2, 1, 3):
             nc.sync.dma_start(
@@ -119,7 +120,7 @@ def tile_list_claim_chart_scores_kernel(
                 nc.vector.tensor_copy(g[:], window.indirect(offs_sb[:]))
                 for c in range(2):
                     picked[a, c] = g[:, c * BANK : (c + 1) * BANK]
-                w_dealt.append(deal_w(a + 1, at(TAB_SC_AT + 2 * H * a, [P, 2 * H], U8, "w_dealt%d" % (a + 1))))
+                w_dealt.append(deal_w(a + 1, at(DEALT_AT + 2 * H * (a + 1), [P, 2 * H], U8, "w_dealt%d" % (a + 1))))
             else:
                 for c in range(2):
                     g = sb([P, BANK], U32, "picked%d_%d" % (a, c))
@@ -267,7 +268,12 @@ def tile_list_claim_chart_scores_kernel(
             gc = sb([P, PACK, width], F32, "g1c%d" % i, tag=tag)
             for t in range(PACK):
                 gather_gain(1, t, gc, pos1_sb[:, m0 // 16 : (m0 + width) // 16], width)
-            x1c.append(weave(gc, width, "x1wc%d" % i))
+            if i < len(chunks) - 1:
+                x1c.append(weave(gc, width, "x1wc%d" % i))
+            else:
+                woven = sb([P, width * PACK], BF16, "x1wc%d" % i)
+                nc.vector.tensor_copy(weave_dst(woven), weave_src(gc))
+                x1c.append(woven)
 
         x1_chunk(0)
         x2q = [quantize(x2w0, NP, "x2q0")]

from contextlib import ExitStack

import concourse.mybir as mybir

K, H, T, S, NP = 1536, 1024, 4096, 1024, 512
FLOPS = 2 * K * H * S + 2 * 2 * H * NP * NP

F32 = mybir.dt.float32
BF16 = mybir.dt.bfloat16
I32 = mybir.dt.int32
U32 = mybir.dt.uint32
U16 = mybir.dt.uint16
U8 = mybir.dt.uint8
FP8X4 = mybir.dt.float8_e4m3fn_x4
FP4X4 = mybir.dt.float4_e2m1fn_x4
ACT = mybir.ActivationFunctionType
ALU = mybir.AluOpType

P = 128
PACK = 4
PASSES1 = K // (P * PACK)
PASSES2 = H // (P * PACK)
BANK = 512
SCALE_ROWS = 16
ROW0 = 36
ROW1 = ROW0 + 2 * SCALE_ROWS
RUN = 4
PAIRS = 3
TAB_BYTES = 4 * T
PICKED0_AT = 3 * TAB_BYTES
DEALT_AT = PICKED0_AT + 4 * S
TAB_SC_AT = DEALT_AT + H
W_RAW_AT = DEALT_AT + PASSES1 * 2 * H


def tile_list_claim_chart_scores_kernel(
    tc, tab_words, tab_scales, offs, pos1, pos2, w4_words, w4_scales, gain, dep, disc, col, row, out
):
    nc = tc.nc
    with ExitStack() as ctx:
        lists = ctx.enter_context(tc.tile_pool(name="lists", bufs=1))
        keep = ctx.enter_context(tc.tile_pool(name="keep", bufs=1))
        laid = ctx.enter_context(tc.tile_pool(name="laid", bufs=1))
        psum = ctx.enter_context(tc.psum_pool(name="psum", bufs=1))

        def sb(shape, dtype, name, tag=None):
            return keep.tile(shape, dtype, name=name, tag=tag or name, align_bytes=64)

        def at(offset, shape, dtype, name):
            return laid.tile(shape, dtype, name=name, offset=offset, align_bytes=64)

        def bank(i, name):
            return psum.tile([P, BANK], F32, name=name, tag="bank%d" % i)

        offs_sb = lists.tile([P, S // 16], U16, name="offs_sb")
        pos1_sb = lists.tile([P, NP // 16], U16, name="pos1_sb")
        pos2_sb = lists.tile([P, NP // 16], U16, name="pos2_sb")
        nc.sync.dma_start(offs_sb[:], offs)
        w_raw = at(W_RAW_AT, [P, PASSES1, 2 * H], U8, "w_raw")
        nc.sync.dma_start(w_raw[:].bitcast(I32), w4_words.rearrange("a p c -> p a c").bitcast(I32))
        nc.sync.dma_start(pos1_sb[:], pos1)
        nc.sync.dma_start(pos2_sb[:], pos2)

        def load_scale_rows(tile, rows):
            nc.vector.memset(tile[:].bitcast(I32), 0)
            nc.sync.dma_start(
                tile[ROW0:ROW1, :].bitcast(I32), rows[0:2].rearrange("a q n -> q a n").bitcast(I32)
            )
            nc.sync.dma_start(tile[ROW1 : ROW1 + SCALE_ROWS, :].bitcast(I32), rows[2].bitcast(I32))

        tab_sc = at(TAB_SC_AT, [P, T], U8, "tab_sc")
        load_scale_rows(tab_sc, tab_scales)
        w_sc = at(2 * TAB_BYTES, [P, H], U8, "w_sc")
        load_scale_rows(w_sc, w4_scales)
        planes = sb([P, PASSES1 * (S + H)], U8, "planes")
        nc.vector.memset(planes[:].bitcast(I32), 0)


        def load_tab(a):
            words = at(a * TAB_BYTES, [P, T], I32, "tab%d" % a)
            nc.sync.dma_start(words[:], tab_words[a].rearrange("p t i -> p (t i)").bitcast(I32))
            return words

        tabs = [load_tab(0), load_tab(1)]

        def deal_w(a, dealt):
            nc.vector.tensor_copy(
                dealt[:].bitcast(U16).rearrange("p (b t q) -> p b t q", b=PASSES2, t=PACK),
                w_raw[:, a, :].bitcast(U16).rearrange("p (b q t) -> p b t q", b=PASSES2, t=PACK),
            )
            return dealt

        picked_sc = at(PICKED0_AT - S // 2, [P, S], U8, "picked_sc")
        nc.vector.tensor_copy(picked_sc[:], tab_sc[:].indirect(offs_sb[:]))
        stage = sb([P, S + H], U8, "stage")
        nc.vector.tensor_copy(
            stage[:, S:].rearrange("p (b t q) -> p b t q", b=PASSES2, t=PACK),
            w_sc[:].rearrange("p (b q t) -> p b t q", b=PASSES2, t=PACK),
        )
        nc.vector.tensor_copy(stage[:, :S].bitcast(I32), picked_sc[:].bitcast(I32))
        w_dealt = [deal_w(0, at(DEALT_AT, [P, 2 * H], U8, "w_dealt0"))]
        pair = 2 * (S + H)
        for quad in (0, 2, 1, 3):
            nc.sync.dma_start(
                planes[32 * quad : 32 * quad + 4, :pair].bitcast(I32).rearrange("r (a n) -> r a n", a=2),
                stage[ROW0 + 8 * quad : ROW0 + 8 * (quad + 1), :].bitcast(I32),
            )
        tabs.append(load_tab(2))
        for quad in (0, 2, 1, 3):
            nc.sync.dma_start(
                planes[32 * quad : 32 * quad + 4, pair:].bitcast(I32),
                stage[ROW1 + 4 * quad : ROW1 + 4 * (quad + 1), :].bitcast(I32),
            )

        picked = {}
        for a in range(PASSES1):
            window = tabs[a][:].bitcast(U32)
            if a < PASSES1 - 1:
                g = at(PICKED0_AT, [P, S], U32, "picked0") if a == 0 else sb([P, S], U32, "picked%d" % a)
                nc.vector.tensor_copy(g[:], window.indirect(offs_sb[:]))
                for c in range(2):
                    picked[a, c] = g[:, c * BANK : (c + 1) * BANK]
                w_dealt.append(deal_w(a + 1, at(DEALT_AT + 2 * H * (a + 1), [P, 2 * H], U8, "w_dealt%d" % (a + 1))))
            else:
                for c in range(2):
                    g = sb([P, BANK], U32, "picked%d_%d" % (a, c))
                    nc.vector.tensor_copy(g[:], window.indirect(offs_sb[:, c * 32 : (c + 1) * 32]))
                    picked[a, c] = g[:]

        gain_sb = at(W_RAW_AT, [P, PASSES2, PACK], F32, "gain_sb")
        disc_sb = at(W_RAW_AT + 64, [P, PASSES2, PACK], F32, "disc_sb")
        nc.sync.dma_start(gain_sb[:], gain.rearrange("(b p t) -> p b t", p=P, t=PACK))
        nc.sync.dma_start(disc_sb[:], disc.rearrange("(b p t) -> p b t", p=P, t=PACK))

        def gain_rows(b, width):
            return gain_sb[:, b, :].unsqueeze(2).broadcast_to([P, PACK, width])

        gain_wide = [sb([P, PACK, NP], F32, "gain_wide0"), sb([P, PACK, NP // 2], F32, "gain_wide1")]
        nc.vector.tensor_copy(gain_wide[0][:], gain_rows(0, NP))
        mag = sb([P, PASSES2 * PACK], F32, "mag")
        gain_flat = gain_sb[:].rearrange("p b t -> p (b t)")
        nc.vector.scalar_tensor_tensor(mag[:], gain_flat, -1.0, gain_flat, ALU.mult, ALU.max)
        weight2 = sb([P, PASSES2, PACK], F32, "weight2")
        nc.vector.tensor_tensor(
            weight2[:].rearrange("p b t -> p (b t)"), mag[:], disc_sb[:].rearrange("p b t -> p (b t)"), ALU.mult
        )

        dep_raw = []
        for b in range(PASSES2):
            raw = at(W_RAW_AT + 128 if b == 0 else 2 * TAB_BYTES, [P, PACK, NP], F32, "dep_raw%d" % b)
            nc.sync.dma_start(raw[:], dep[b * P * PACK : (b + 1) * P * PACK, :].rearrange("(p t) m -> p t m", t=PACK))
            dep_raw.append(raw)

        def mm1(acc, b, t, a, c):
            base = a * (S + H)
            wtile = b * P * PACK + t * P
            wcol = base + S + wtile
            nc.tensor.matmul_mx(
                acc[:],
                lhsT=w_dealt[a][:, 2 * wtile : 2 * (wtile + P)].bitcast(FP4X4),
                lhsT_scale=planes[:, wcol : wcol + P],
                rhs=picked[a, c].bitcast(FP8X4),
                rhs_scale=planes[:, base + c * BANK : base + (c + 1) * BANK],
                start=(a == 0),
                stop=(a == PASSES1 - 1),
            )

        th = {}

        def tanh_tile(b, t, accs):
            th[b, t] = sb([P, S], F32, "th%d_%d" % (b, t))
            for c in range(2):
                nc.scalar.activation(th[b, t][:, c * BANK : (c + 1) * BANK], accs[c][:], ACT.Tanh)

        def stage1_tile(b, t):
            accs = [bank(2 * ((PACK * b + t) % PAIRS) + c, "acc%d_%d_%d" % (b, t, c)) for c in range(2)]
            for c in range(2):
                for a in range(PASSES1):
                    mm1(accs[c], b, t, a, c)
            tanh_tile(b, t, accs)

        def weave_dst(tile):
            return tile[:].rearrange("p (c i t) -> p c t i", i=RUN, t=PACK)

        def weave_src(tile):
            return tile[:].rearrange("p t (c i) -> p c t i", i=RUN)

        def quantize(woven, width, name):
            codes = sb([P, width], U32, name + "_codes")
            scales = sb([P, width], U8, name + "_scales")
            nc.vector.quantize_mx(codes[:].bitcast(FP8X4), scales[:], woven[:])
            return codes, scales

        def gather(b, t, dst, offsets):
            nc.vector.tensor_copy(dst[:, t, :], th[b, t][:].indirect(offsets))

        def x2_abs(b, g2):
            mags = sb([P, NP * PACK], F32, "mags%d" % b, tag="mags")
            nc.scalar.activation(weave_dst(mags), weave_src(g2), ACT.Abs)
            return mags

        def x2_round(b, mags):
            woven = sb([P, NP * PACK], BF16, "x2w%d" % b)
            nc.vector.tensor_tensor(
                woven[:].rearrange("p (n t) -> p n t", t=PACK),
                mags[:].rearrange("p (n t) -> p n t", t=PACK),
                weight2[:, b : b + 1, :].broadcast_to([P, NP, PACK]),
                ALU.mult,
            )
            return woven

        def gather_gain(b, t, dst, offsets, width):
            nc.vector.tensor_tensor(
                dst[:, t, :], th[b, t][:].indirect(offsets), gain_wide[b][:, t, :width], ALU.mult
            )

        def weave(src, width, name, tag=None):
            woven = sb([P, width * PACK], BF16, name, tag=tag)
            nc.scalar.copy(weave_dst(woven), weave_src(src))
            return woven

        accs0 = {(t, c): bank(2 * t + c, "acc0_%d_%d" % (t, c)) for t in range(PAIRS) for c in range(2)}
        for a in range(PASSES1 - 1):
            for t in range(PAIRS):
                for c in range(2):
                    mm1(accs0[t, c], 0, t, a, c)
        for c in range(2):
            for t in range(PAIRS):
                mm1(accs0[t, c], 0, t, PASSES1 - 1, c)
        row_sb = at(2 * TAB_BYTES + TAB_BYTES // 2, [P, NP], F32, "row_sb")
        nc.sync.dma_start(row_sb[:], row.partition_broadcast(P))
        col_sb = at(2 * TAB_BYTES + TAB_BYTES // 2 + 4 * NP, [P, NP // P], F32, "col_sb")
        with nc.allow_non_contiguous_dma(reason="one value of col to a partition"):
            nc.sync.dma_start(col_sb[:], col.rearrange("(i p) -> p i", p=P))

        g2 = [sb([P, PACK, NP], F32, "g2_%d" % b) for b in range(PASSES2)]
        g1 = sb([P, PACK, NP], F32, "g1_0")
        for t in range(PACK):
            if t < PAIRS:
                tanh_tile(0, t, [accs0[t, 0], accs0[t, 1]])
            else:
                stage1_tile(0, t)
            gather(0, t, g2[0], pos2_sb[:])
        for t in range(PACK):
            gather_gain(0, t, g1, pos1_sb[:], NP)
        for t in range(PACK):
            stage1_tile(1, t)
            gather(1, t, g2[1], pos2_sb[:])
        depw = [weave(dep_raw[0], NP, "depw0", tag="th0_0")]
        mags0 = sb([P, PACK, NP], F32, "mags0")
        nc.scalar.activation(mags0[:], g2[0][:], ACT.Abs)
        x1w = weave(g1, NP, "x1w0")
        rounded = sb([P, PACK, NP], BF16, "rounded")
        for t in range(PACK):
            nc.vector.tensor_scalar(rounded[:, t, :], mags0[:, t, :], weight2[:, 0, t : t + 1], None, ALU.mult)
        depq = [quantize(depw[0], NP, "depq0")]
        x1q0 = quantize(x1w, NP, "x1q0")
        nc.scalar.copy(gain_wide[1][:], gain_rows(1, NP // 2))
        x2w0 = weave(rounded, NP, "x2w0")
        mags = x2_abs(1, g2[1])
        depw.append(weave(dep_raw[1], NP, "depw1", tag="th0_1"))

        chunks = [(0, 256, "mags0"), (256, 128, "x2w0"), (384, 128, "x2w1")]
        x1c = []

        def x1_chunk(i):
            m0, width, tag = chunks[i]
            gc = sb([P, PACK, width], F32, "g1c%d" % i, tag=tag)
            for t in range(PACK):
                gather_gain(1, t, gc, pos1_sb[:, m0 // 16 : (m0 + width) // 16], width)
            if i < len(chunks) - 1:
                x1c.append(weave(gc, width, "x1wc%d" % i))
            else:
                woven = sb([P, width * PACK], BF16, "x1wc%d" % i)
                nc.vector.tensor_copy(weave_dst(woven), weave_src(gc))
                x1c.append(woven)

        x1_chunk(0)
        x2q = [quantize(x2w0, NP, "x2q0")]
        x1_chunk(1)
        x2q.append(quantize(x2_round(1, mags), NP, "x2q1"))
        depq.append(quantize(depw[1], NP, "depq1"))

        parts = [(i, 0, NP) for i in range(NP // P - 1)] + [(NP // P - 1, j0, NP // 2) for j0 in (0, NP // 2)]
        scores = [
            psum.tile([P, width], F32, name="score%d" % n, tag="bank%d" % ((2 * PAIRS + n) % 8))
            for n, (i, j0, width) in enumerate(parts)
        ]

        def mm2(n, lhs, m0, rhs, start, stop):
            i, j0, width = parts[n]
            nc.tensor.matmul_mx(
                scores[n][:],
                lhsT=lhs[0][:, i * P - m0 : (i + 1) * P - m0].bitcast(FP8X4),
                lhsT_scale=lhs[1][:, i * P - m0 : (i + 1) * P - m0],
                rhs=rhs[0][:, j0 : j0 + width].bitcast(FP8X4),
                rhs_scale=rhs[1][:, j0 : j0 + width],
                start=start,
                stop=stop,
            )

        for n in range(len(parts)):
            mm2(n, x1q0, 0, x2q[0], True, False)
        for b in range(PASSES2):
            for n in range(len(parts)):
                mm2(n, depq[b], 0, x2q[b], False, False)
        for ci, (m0, count, tag) in enumerate(chunks):
            if ci == 1:
                x1_chunk(2)
            x1q = quantize(x1c[ci], count, "x1qc%d" % ci)
            for n, (i, j0, width) in enumerate(parts):
                if m0 <= i * P < m0 + count:
                    mm2(n, x1q, m0, x2q[1], False, True)
                    te = sb([P, width], F32, "te%d" % n)
                    nc.scalar.activation(te[:], scores[n][:], ACT.Tanh)
                    res = sb([P, width], F32, "res%d" % n)
                    nc.vector.scalar_tensor_tensor(
                        res[:], te[:], col_sb[:, i : i + 1], row_sb[:, j0 : j0 + width], ALU.mult, ALU.add
                    )
                    nc.sync.dma_start(out[i * P : (i + 1) * P, j0 : j0 + width], res[:])
